import numpy as np, ml_dtypes
CORES = [7,15,23,39,47,63,71,79,87,95,119,127]
N = 12
import mx_ref
NC = 256
CNT = [[16,8,32,8,16,8,16,8,64,48,0,32],[8,8,16,0,24,40,16,0,72,64,8,0],[0,16,96,32,0,56,40,8,0,0,8,0],[0,8,0,80,0,0,0,24,24,32,88,0],[0,16,40,0,0,32,0,16,32,24,32,64],[48,72,24,0,32,80,0,0,0,0,0,0],[16,0,8,8,104,16,16,24,0,8,0,56],[8,0,8,64,0,0,16,56,0,0,88,16],[0,64,0,0,56,8,8,8,16,32,0,64],[72,48,0,0,0,8,96,0,8,16,0,8],[0,16,16,64,8,0,8,80,16,32,0,16],[88,0,16,0,16,8,40,32,24,0,32,0]]
OFF = [[sum(c[:e]) for e in range(N + 1)] for c in CNT]
BF = ml_dtypes.bfloat16
def setup_inputs(rng):
    def f(*shape):
        return mx_ref.flush((rng.standard_normal(shape, dtype=np.float32) * np.exp2(rng.integers(-2, 3, shape[:-1] + (1,)))).astype(BF))
    return {"w": f(N, 128, 512), "x": f(N, 128, 4 * NC)}
def setup_inputs_blocks(rng):
    d = setup_inputs(rng)
    for k in ("w", "x"): d[k] = mx_ref.spread(d[k], rng, 4)
    return d
def setup_inputs_wide(rng):
    d = setup_inputs(rng)
    for k in ("w", "x"): d[k] = mx_ref.flush((d[k].astype(np.float32) * np.exp2(rng.integers(-8, 9, (N, 1, 1))).astype(np.float32)).astype(BF))
    return d
def setup_inputs_zeros(rng):
    d = setup_inputs(rng); v = d["x"].reshape(N, 128, -1, 4).copy()
    v[np.broadcast_to((rng.random((N, 1, v.shape[2], 1)) < 0.33), v.shape)] = 0
    d["x"] = v.reshape(d["x"].shape)
    return d
def reference(w, x):
    y = np.zeros((N, 128, NC), np.float32)
    for e in range(N):
        t = np.concatenate([x[j][:, 4 * OFF[j][e]:4 * OFF[j][e + 1]] for j in range(N)], axis=1)
        y[e] = mx_ref.matmul(mx_ref.quantize(w[e]), mx_ref.quantize(t))
    return {"y": y}

@@ -1,0 +1,137 @@
+from concourse.bass import DstId, RemoteDMATransfer
+from concourse.mybir import dt
+
+NCOL = 256
+WCOL = 128
+
+SCRATCH = {
+    "xs": ("sbuf", [128, 4 * NCOL], "bfloat16"),
+    "ws": ("sbuf", [128, 4 * WCOL], "bfloat16"),
+    "xq": ("sbuf", [128, NCOL], "float8_e4m3fn_x4"),
+    "xp": ("sbuf", [128, NCOL], "uint8"),
+    "wq": ("sbuf", [128, WCOL], "float8_e4m3fn_x4"),
+    "wp": ("sbuf", [128, WCOL], "uint8"),
+    "bq": ("sbuf", [128, NCOL], "float8_e4m3fn_x4"),
+    "bp": ("sbuf", [128, NCOL], "uint8"),
+    "pa": ("psum", [128, 512], "float32"),
+    "pb": ("psum", [128, 512], "float32"),
+    "ys": ("sbuf", [128, NCOL], "float32"),
+}
+SEMAPHORES = ["xl", "wl", "xd", "wd", "arr", "sent", "ma", "mb", "cp", "st"]
+
+
+def _share(k, n_eng):
+    p = 1
+    while p * 2 * k <= n_eng:
+        p *= 2
+    m = [p] * k
+    left = n_eng - p * k
+    i = 0
+    while i < k and left >= m[i]:
+        left -= m[i]
+        m[i] *= 2
+        i += 1
+    return m
+
+
+def _plan(T, topo):
+    cnt = T.tables["CNT"]
+    cores = T.cores
+    n = len(cores)
+    off = [[sum(cnt[j][:e]) for e in range(n + 1)] for j in range(n)]
+    pos = [[sum(cnt[i][e] for i in range(j) if i != e) for e in range(n)] for j in range(n)]
+    calls = [[] for _ in range(n)]
+    arrive = [0] * n
+    sent = [0] * n
+    for j in range(n):
+        groups = {}
+        common = None
+        for e in range(n):
+            c = cnt[j][e]
+            if e == j or c == 0:
+                continue
+            groups.setdefault(4 * c, []).append((e, "q"))
+            groups.setdefault(c, []).append((e, "p"))
+            m = topo.mask(cores[j], cores[e])
+            common = m if common is None else (common & m)
+        if common is None:
+            continue
+        engines = [i for i in range(common.bit_length()) if (common >> i) & 1]
+        load = dict((i, 0) for i in engines)
+        for width in sorted(groups, reverse=True):
+            todo = groups[width]
+            while todo:
+                now, todo = todo[:len(engines)], todo[len(engines):]
+                free = sorted(engines, key=lambda i: (load[i], i))
+                call = []
+                for (e, kind), m in zip(now, sorted(_share(len(now), len(engines)))):
+                    use, free = free[:m], free[m:]
+                    for i in use:
+                        load[i] += 128 // m
+                    call.append((e, kind, off[j][e], pos[j][e], cnt[j][e], sum(1 << i for i in use), m))
+                    arrive[e] += m
+                    sent[j] += m
+                calls[j].append(call)
+    return calls, arrive, sent
+
+
+def rank_program(g, core, T, topo):
+    rank = T.rank_of(core)
+    if rank is None:
+        return
+    S = T.sem
+    cnt = T.tables["CNT"]
+    n = len(T.cores)
+    calls, arrive, sent = _plan(T, topo)
+    own = cnt[rank][rank]
+    own_at = sum(cnt[rank][:rank])
+    before = sum(cnt[i][rank] for i in range(rank))
+    landed = NCOL - own
+
+    g.sync.dma_start(T.xs[:], T.x[:]).then_inc(S.xl, 16)
+    g.scalar.wait_ge(S.xl, 16)
+    g.scalar.dma_start(T.ws[:], T.w[:]).then_inc(S.wl, 16)
+
+    g.vector.wait_ge(S.xl, 16)
+    g.vector.quantize_mx(T.xq[:], T.xp[:], T.xs[:]).then_inc(S.xd, 1)
+    g.vector.wait_ge(S.wl, 16)
+    g.vector.quantize_mx(T.wq[:], T.wp[:], T.ws[:]).then_inc(S.wd, 1)
+
+    g.wait_ge(S.xd, 1)
+    for call in calls[rank]:
+        trs = []
+        for (e, kind, s0, d0, c, mask, m) in call:
+            rid, pid, _ = topo.addr(T.cores[e])
+            if kind == "q":
+                src = T.xq[:, s0:s0 + c].bitcast(dt.uint8)
+                dst = T.bq[:, d0:d0 + c].bitcast(dt.uint8)
+            else:
+                src = T.xp[:, s0:s0 + c]
+                dst = T.bp[:, d0:d0 + c]
+            trs.append(RemoteDMATransfer(dst_ids=[DstId(rid=rid, pnc=pid)], dma_engine_mask=mask,
+                                         remote_sem=S.arr, src=src, dst=dst))
+        g.remote_dma_fused(trs, local_sem=S.sent)
+
+    copies = 0
+    g.tensor.wait_ge(S.wd, 1)
+    if own:
+        g.tensor.wait_ge(S.xd, 1)
+        g.tensor.matmul_mx(T.pa[:, 0:NCOL], T.wq[:], T.wp[:], T.xq[:], T.xp[:], True, True).then_inc(S.ma, 1)
+        g.vector.wait_ge(S.ma, 1)
+        g.vector.tensor_copy(T.ys[:, before:before + own], T.pa[:, own_at:own_at + own]).then_inc(S.cp, 1)
+        copies += 1
+    g.tensor.wait_ge(S.arr, arrive[rank])
+    g.tensor.matmul_mx(T.pb[:, 0:landed], T.wq[:], T.wp[:], T.bq[:, 0:landed], T.bp[:, 0:landed],
+                       True, True).then_inc(S.mb, 1)
+    g.vector.wait_ge(S.mb, 1)
+    if before:
+        g.vector.tensor_copy(T.ys[:, 0:before], T.pb[:, 0:before]).then_inc(S.cp, 1)
+        copies += 1
+    if before < landed:
+        g.vector.tensor_copy(T.ys[:, before + own:NCOL], T.pb[:, before:landed]).then_inc(S.cp, 1)
+        copies += 1
+    g.sync.wait_ge(S.cp, copies)
+    g.sync.dma_start(T.y[:], T.ys[:]).then_inc(S.st, 16)
+    g.sync.wait_ge(S.st, 16)
+    if sent[rank]:
+        g.wait_ge(S.sent, sent[rank])

@@ -3,6 +3,8 @@ from concourse.mybir import dt
 
 NCOL = 256
 WCOL = 128
+HALF = 128
+ROW = 128
 
 SCRATCH = {
     "xs": ("sbuf", [128, 4 * NCOL], "bfloat16"),
@@ -15,9 +17,11 @@ SCRATCH = {
     "bp": ("sbuf", [128, NCOL], "uint8"),
     "pa": ("psum", [128, 512], "float32"),
     "pb": ("psum", [128, 512], "float32"),
+    "pc": ("psum", [128, 512], "float32"),
     "ys": ("sbuf", [128, NCOL], "float32"),
 }
-SEMAPHORES = ["xl", "wl", "xd", "wd", "arr", "sent", "ma", "mb", "cp", "st"]
+SEMAPHORES = ["xl0", "xl1", "wl", "xd0", "xd1", "wd", "arr", "sent", "ma", "mb", "mc", "cp0", "cp1", "st0", "st1"]
+_CACHE = {}
 
 
 def _share(k, n_eng):
@@ -41,6 +45,7 @@ def _plan(T, topo):
     off = [[sum(cnt[j][:e]) for e in range(n + 1)] for j in range(n)]
     pos = [[sum(cnt[i][e] for i in range(j) if i != e) for e in range(n)] for j in range(n)]
     calls = [[] for _ in range(n)]
+    first = [0] * n
     arrive = [0] * n
     sent = [0] * n
     for j in range(n):
@@ -57,8 +62,19 @@ def _plan(T, topo):
         if common is None:
             continue
         engines = [i for i in range(common.bit_length()) if (common >> i) & 1]
-        load = dict((i, 0) for i in engines)
+        lead = None
         for width in sorted(groups, reverse=True):
+            for h in (0, 1):
+                if lead is None and len(groups[width]) <= len(engines) and all(
+                        h * HALF <= off[j][e] and off[j][e + 1] <= (h + 1) * HALF for e, _ in groups[width]):
+                    lead = (width, h)
+        order = sorted(groups, reverse=True)
+        if lead is not None:
+            first[j] = lead[1]
+            order.remove(lead[0])
+            order.insert(0, lead[0])
+        load = dict((i, 0) for i in engines)
+        for width in order:
             todo = groups[width]
             while todo:
                 now, todo = todo[:len(engines)], todo[len(engines):]
@@ -67,38 +83,44 @@ def _plan(T, topo):
                 for (e, kind), m in zip(now, sorted(_share(len(now), len(engines)))):
                     use, free = free[:m], free[m:]
                     for i in use:
-                        load[i] += 128 // m
+                        load[i] += (128 // m) * (ROW + width)
                     call.append((e, kind, off[j][e], pos[j][e], cnt[j][e], sum(1 << i for i in use), m))
                     arrive[e] += m
                     sent[j] += m
                 calls[j].append(call)
-    return calls, arrive, sent
+        if lead is None:
+            calls[j].insert(0, [])
+    return first, calls, arrive, sent
 
 
 def rank_program(g, core, T, topo):
     rank = T.rank_of(core)
     if rank is None:
         return
+    if "plan" not in _CACHE:
+        _CACHE["plan"] = _plan(T, topo)
+    first, calls, arrive, sent = _CACHE["plan"]
     S = T.sem
     cnt = T.tables["CNT"]
-    n = len(T.cores)
-    calls, arrive, sent = _plan(T, topo)
     own = cnt[rank][rank]
     own_at = sum(cnt[rank][:rank])
     before = sum(cnt[i][rank] for i in range(rank))
     landed = NCOL - own
 
-    g.sync.dma_start(T.xs[:], T.x[:]).then_inc(S.xl, 16)
-    g.scalar.wait_ge(S.xl, 16)
-    g.scalar.dma_start(T.ws[:], T.w[:]).then_inc(S.wl, 16)
-
-    g.vector.wait_ge(S.xl, 16)
-    g.vector.quantize_mx(T.xq[:], T.xp[:], T.xs[:]).then_inc(S.xd, 1)
+    for i, h in enumerate((first[rank], 1 - first[rank])):
+        g.sync.dma_start(T.xs[:, 4 * h * HALF:4 * (h + 1) * HALF],
+                         T.x[:, 4 * h * HALF:4 * (h + 1) * HALF]).then_inc(S["xl%d" % i], 16)
+        g.vector.wait_ge(S["xl%d" % i], 16)
+        g.vector.quantize_mx(T.xq[:, h * HALF:(h + 1) * HALF], T.xp[:, h * HALF:(h + 1) * HALF],
+                             T.xs[:, 4 * h * HALF:4 * (h + 1) * HALF]).then_inc(S["xd%d" % i], 1)
+    g.sync.dma_start(T.ws[:], T.w[:]).then_inc(S.wl, 16)
     g.vector.wait_ge(S.wl, 16)
     g.vector.quantize_mx(T.wq[:], T.wp[:], T.ws[:]).then_inc(S.wd, 1)
 
-    g.wait_ge(S.xd, 1)
-    for call in calls[rank]:
+    g.wait_ge(S.xd0, 1)
+    for i, call in enumerate(calls[rank]):
+        if i == 1:
+            g.wait_ge(S.xd1, 1)
         trs = []
         for (e, kind, s0, d0, c, mask, m) in call:
             rid, pid, _ = topo.addr(T.cores[e])
@@ -110,28 +132,48 @@ def rank_program(g, core, T, topo):
                 dst = T.bp[:, d0:d0 + c]
             trs.append(RemoteDMATransfer(dst_ids=[DstId(rid=rid, pnc=pid)], dma_engine_mask=mask,
                                          remote_sem=S.arr, src=src, dst=dst))
-        g.remote_dma_fused(trs, local_sem=S.sent)
+        if trs:
+            g.remote_dma_fused(trs, local_sem=S.sent)
+    if len(calls[rank]) < 2:
+        g.wait_ge(S.xd1, 1)
 
-    copies = 0
+    cut = landed
+    if landed >= HALF + HALF // 2:
+        cut = landed // 16 * 8
+        if own and 0 < before < landed and abs(before - cut) <= 48:
+            cut = before
+    ycut = cut if cut < before else cut + own
+    parts = [(0, cut, 0, max(cut, HALF), T.pb, S.mb), (cut, landed, min(cut, landed - HALF), landed, T.pc, S.mc)]
+    copies = [0, 0]
+
     g.tensor.wait_ge(S.wd, 1)
     if own:
-        g.tensor.wait_ge(S.xd, 1)
+        g.tensor.wait_ge(S.xd0, 1)
+        g.tensor.wait_ge(S.xd1, 1)
         g.tensor.matmul_mx(T.pa[:, 0:NCOL], T.wq[:], T.wp[:], T.xq[:], T.xp[:], True, True).then_inc(S.ma, 1)
+        p = 0 if before < ycut else 1
         g.vector.wait_ge(S.ma, 1)
-        g.vector.tensor_copy(T.ys[:, before:before + own], T.pa[:, own_at:own_at + own]).then_inc(S.cp, 1)
-        copies += 1
+        g.vector.tensor_copy(T.ys[:, before:before + own], T.pa[:, own_at:own_at + own]).then_inc(S["cp%d" % p], 1)
+        copies[p] += 1
     g.tensor.wait_ge(S.arr, arrive[rank])
-    g.tensor.matmul_mx(T.pb[:, 0:landed], T.wq[:], T.wp[:], T.bq[:, 0:landed], T.bp[:, 0:landed],
-                       True, True).then_inc(S.mb, 1)
-    g.vector.wait_ge(S.mb, 1)
-    if before:
-        g.vector.tensor_copy(T.ys[:, 0:before], T.pb[:, 0:before]).then_inc(S.cp, 1)
-        copies += 1
-    if before < landed:
-        g.vector.tensor_copy(T.ys[:, before + own:NCOL], T.pb[:, before:landed]).then_inc(S.cp, 1)
-        copies += 1
-    g.sync.wait_ge(S.cp, copies)
-    g.sync.dma_start(T.y[:], T.ys[:]).then_inc(S.st, 16)
-    g.sync.wait_ge(S.st, 16)
+    for p, (lo, hi, w0, w1, bank, sem) in enumerate(parts):
+        if lo == hi:
+            continue
+        g.tensor.matmul_mx(bank[:, 0:w1 - w0], T.wq[:], T.wp[:], T.bq[:, w0:w1], T.bp[:, w0:w1],
+                           True, True).then_inc(sem, 1)
+        g.vector.wait_ge(sem, 1)
+        mid = before if (own and lo < before < hi) else hi
+        for a, b in ((lo, mid), (mid, hi)):
+            if a == b:
+                continue
+            ya = a if a < before else a + own
+            g.vector.tensor_copy(T.ys[:, ya:ya + b - a], bank[:, a - w0:b - w0]).then_inc(S["cp%d" % p], 1)
+            copies[p] += 1
+    for p, q, (ya, yb) in ((0, g.sync, (0, ycut)), (1, g.scalar, (ycut, NCOL))):
+        if ya == yb:
+            continue
+        q.wait_ge(S["cp%d" % p], copies[p])
+        q.dma_start(T.y[:, ya:yb], T.ys[:, ya:yb]).then_inc(S["st%d" % p], 16)
+        q.wait_ge(S["st%d" % p], 16)
     if sent[rank]:
         g.wait_ge(S.sent, sent[rank])

from concourse.bass import DstId, RemoteDMATransfer
from concourse.mybir import dt

NCOL = 256
WCOL = 128
HALF = 128
ROW = 128

SCRATCH = {
    "xs": ("sbuf", [128, 4 * NCOL], "bfloat16"),
    "ws": ("sbuf", [128, 4 * WCOL], "bfloat16"),
    "xq": ("sbuf", [128, NCOL], "float8_e4m3fn_x4"),
    "xp": ("sbuf", [128, NCOL], "uint8"),
    "wq": ("sbuf", [128, WCOL], "float8_e4m3fn_x4"),
    "wp": ("sbuf", [128, WCOL], "uint8"),
    "bq": ("sbuf", [128, NCOL], "float8_e4m3fn_x4"),
    "bp": ("sbuf", [128, NCOL], "uint8"),
    "pa": ("psum", [128, 512], "float32"),
    "pb": ("psum", [128, 512], "float32"),
    "pc": ("psum", [128, 512], "float32"),
    "ys": ("sbuf", [128, NCOL], "float32"),
}
SEMAPHORES = ["xl0", "xl1", "wl", "xd0", "xd1", "wd", "arr", "sent", "ma", "mb", "mc", "cp0", "cp1", "st0", "st1"]
_CACHE = {}


def _share(k, n_eng):
    p = 1
    while p * 2 * k <= n_eng:
        p *= 2
    m = [p] * k
    left = n_eng - p * k
    i = 0
    while i < k and left >= m[i]:
        left -= m[i]
        m[i] *= 2
        i += 1
    return m


def _plan(T, topo):
    cnt = T.tables["CNT"]
    cores = T.cores
    n = len(cores)
    off = [[sum(cnt[j][:e]) for e in range(n + 1)] for j in range(n)]
    pos = [[sum(cnt[i][e] for i in range(j) if i != e) for e in range(n)] for j in range(n)]
    calls = [[] for _ in range(n)]
    first = [0] * n
    arrive = [0] * n
    sent = [0] * n
    for j in range(n):
        groups = {}
        common = None
        for e in range(n):
            c = cnt[j][e]
            if e == j or c == 0:
                continue
            groups.setdefault(4 * c, []).append((e, "q"))
            groups.setdefault(c, []).append((e, "p"))
            m = topo.mask(cores[j], cores[e])
            common = m if common is None else (common & m)
        if common is None:
            continue
        engines = [i for i in range(common.bit_length()) if (common >> i) & 1]
        lead = None
        for width in sorted(groups, reverse=True):
            for h in (0, 1):
                if lead is None and len(groups[width]) <= len(engines) and all(
                        h * HALF <= off[j][e] and off[j][e + 1] <= (h + 1) * HALF for e, _ in groups[width]):
                    lead = (width, h)
        order = sorted(groups, reverse=True)
        if lead is not None:
            first[j] = lead[1]
            order.remove(lead[0])
            order.insert(0, lead[0])
        load = dict((i, 0) for i in engines)
        for width in order:
            todo = groups[width]
            while todo:
                now, todo = todo[:len(engines)], todo[len(engines):]
                free = sorted(engines, key=lambda i: (load[i], i))
                call = []
                for (e, kind), m in zip(now, sorted(_share(len(now), len(engines)))):
                    use, free = free[:m], free[m:]
                    for i in use:
                        load[i] += (128 // m) * (ROW + width)
                    call.append((e, kind, off[j][e], pos[j][e], cnt[j][e], sum(1 << i for i in use), m))
                    arrive[e] += m
                    sent[j] += m
                calls[j].append(call)
        if lead is None:
            calls[j].insert(0, [])
    return first, calls, arrive, sent


def rank_program(g, core, T, topo):
    rank = T.rank_of(core)
    if rank is None:
        return
    if "plan" not in _CACHE:
        _CACHE["plan"] = _plan(T, topo)
    first, calls, arrive, sent = _CACHE["plan"]
    S = T.sem
    cnt = T.tables["CNT"]
    own = cnt[rank][rank]
    own_at = sum(cnt[rank][:rank])
    before = sum(cnt[i][rank] for i in range(rank))
    landed = NCOL - own

    for i, h in enumerate((first[rank], 1 - first[rank])):
        g.sync.dma_start(T.xs[:, 4 * h * HALF:4 * (h + 1) * HALF],
                         T.x[:, 4 * h * HALF:4 * (h + 1) * HALF]).then_inc(S["xl%d" % i], 16)
        g.vector.wait_ge(S["xl%d" % i], 16)
        g.vector.quantize_mx(T.xq[:, h * HALF:(h + 1) * HALF], T.xp[:, h * HALF:(h + 1) * HALF],
                             T.xs[:, 4 * h * HALF:4 * (h + 1) * HALF]).then_inc(S["xd%d" % i], 1)
    g.sync.dma_start(T.ws[:], T.w[:]).then_inc(S.wl, 16)
    g.vector.wait_ge(S.wl, 16)
    g.vector.quantize_mx(T.wq[:], T.wp[:], T.ws[:]).then_inc(S.wd, 1)

    g.wait_ge(S.xd0, 1)
    for i, call in enumerate(calls[rank]):
        if i == 1:
            g.wait_ge(S.xd1, 1)
        trs = []
        for (e, kind, s0, d0, c, mask, m) in call:
            rid, pid, _ = topo.addr(T.cores[e])
            if kind == "q":
                src = T.xq[:, s0:s0 + c].bitcast(dt.uint8)
                dst = T.bq[:, d0:d0 + c].bitcast(dt.uint8)
            else:
                src = T.xp[:, s0:s0 + c]
                dst = T.bp[:, d0:d0 + c]
            trs.append(RemoteDMATransfer(dst_ids=[DstId(rid=rid, pnc=pid)], dma_engine_mask=mask,
                                         remote_sem=S.arr, src=src, dst=dst))
        if trs:
            g.remote_dma_fused(trs, local_sem=S.sent)
    if len(calls[rank]) < 2:
        g.wait_ge(S.xd1, 1)

    cut = landed
    if landed >= HALF + HALF // 2:
        cut = landed // 16 * 8
        if own and 0 < before < landed and abs(before - cut) <= 48:
            cut = before
    ycut = cut if cut < before else cut + own
    parts = [(0, cut, 0, max(cut, HALF), T.pb, S.mb), (cut, landed, min(cut, landed - HALF), landed, T.pc, S.mc)]
    copies = [0, 0]

    g.tensor.wait_ge(S.wd, 1)
    if own:
        g.tensor.wait_ge(S.xd0, 1)
        g.tensor.wait_ge(S.xd1, 1)
        g.tensor.matmul_mx(T.pa[:, 0:NCOL], T.wq[:], T.wp[:], T.xq[:], T.xp[:], True, True).then_inc(S.ma, 1)
        p = 0 if before < ycut else 1
        g.vector.wait_ge(S.ma, 1)
        g.vector.tensor_copy(T.ys[:, before:before + own], T.pa[:, own_at:own_at + own]).then_inc(S["cp%d" % p], 1)
        copies[p] += 1
    g.tensor.wait_ge(S.arr, arrive[rank])
    for p, (lo, hi, w0, w1, bank, sem) in enumerate(parts):
        if lo == hi:
            continue
        g.tensor.matmul_mx(bank[:, 0:w1 - w0], T.wq[:], T.wp[:], T.bq[:, w0:w1], T.bp[:, w0:w1],
                           True, True).then_inc(sem, 1)
        g.vector.wait_ge(sem, 1)
        mid = before if (own and lo < before < hi) else hi
        for a, b in ((lo, mid), (mid, hi)):
            if a == b:
                continue
            ya = a if a < before else a + own
            g.vector.tensor_copy(T.ys[:, ya:ya + b - a], bank[:, a - w0:b - w0]).then_inc(S["cp%d" % p], 1)
            copies[p] += 1
    for p, q, (ya, yb) in ((0, g.sync, (0, ycut)), (1, g.scalar, (ycut, NCOL))):
        if ya == yb:
            continue
        q.wait_ge(S["cp%d" % p], copies[p])
        q.dma_start(T.y[:, ya:yb], T.ys[:, ya:yb]).then_inc(S["st%d" % p], 16)
        q.wait_ge(S["st%d" % p], 16)
    if sent[rank]:
        g.wait_ge(S.sent, sent[rank])
